import numpy as np
import ml_dtypes


def mxq(x, axis, fmt="e4m3"):
    dtype, down = {"e4m3": (ml_dtypes.float8_e4m3fn, 7), "e5m2": (ml_dtypes.float8_e5m2, 14)}[fmt]
    v = np.moveaxis(np.asarray(x, np.float32).astype(ml_dtypes.bfloat16).astype(np.float64), axis, -1)
    blocks = v.reshape(v.shape[:-1] + (-1, 32))
    amax = np.abs(blocks).max(-1, keepdims=True)
    byte = np.maximum(np.where(amax > 0, np.frexp(amax)[1] - 1 + 127, 0) - down, 1)
    scale = np.exp2(byte - 127.0)
    codes = (blocks / scale).astype(np.float32).astype(dtype).astype(np.float64)
    return np.moveaxis((codes * scale).reshape(v.shape), -1, axis)


WIDE = False


def mx_kscale(k):
    if not WIDE:
        return np.ones(k)
    levels = np.array([10, -10, 5, -5, 0])
    if k % 512:
        return np.exp2(np.random.permutation(np.resize(levels, k // 32))).repeat(32)
    a = np.empty((k // 512, 16))
    for p in range(k // 512):
        a[p, :8] = np.random.permutation(np.resize(levels, 8))
        for g in range(8):
            far = levels[np.abs(levels - a[p, g]) >= 10]
            a[p, g + 8] = far[np.random.randint(len(far))]
    return np.exp2(a.ravel()).repeat(32)


def f64(x):
    return np.asarray(x).astype(np.float64)


def striped(idx):
    return np.tile(np.asarray(idx).reshape(-1, 16).T, (8, 1)).astype(np.uint16)


def unstriped(offs):
    return offs[:16].T.reshape(-1).astype(np.int64)


E2M1 = np.array([0.0, 0.5, 1.0, 1.5, 2.0, 3.0, 4.0, 6.0, -0.0, -0.5, -1.0, -1.5, -2.0, -3.0, -4.0, -6.0])


def pack_weight(w, fmt):
    k, n = w.shape
    w = f64(np.asarray(w, np.float32).astype(ml_dtypes.bfloat16)).reshape(k // 32, 32, n)
    amax = np.abs(w).max(1)
    if fmt == "e4m3":
        byte = np.frexp(amax)[1] - 1 + 127 - 7
    else:
        mant, ex = np.frexp(amax / 6.0)
        byte = np.where(mant > 0.5, ex, ex - 1) + 127
    byte = np.clip(np.where(amax > 0, byte, 1), 1, 254)
    scaled = (w * np.exp2(127.0 - byte)[:, None, :]).reshape(k, n).astype(np.float32)
    by_word = np.ascontiguousarray(scaled.reshape(k // 512, 128, 4, n).transpose(0, 1, 3, 2))
    if fmt == "e4m3":
        words = by_word.astype(ml_dtypes.float8_e4m3fn).view(np.uint8)
    else:
        c = by_word.astype(ml_dtypes.float4_e2m1fn).view(np.uint8) & 0xF
        words = (c[..., 0::2] | (c[..., 1::2] << 4)).reshape(k // 512, 128, 2 * n)
    return np.ascontiguousarray(words), np.ascontiguousarray(byte.astype(np.uint8).reshape(k // 512, 16, n))


def unpack_weight(words, scales, fmt):
    g, _, n = scales.shape
    words = np.ascontiguousarray(words).reshape(g, 128, n, -1)
    if fmt == "e4m3":
        vals = words.view(ml_dtypes.float8_e4m3fn).astype(np.float64)
    else:
        nib = np.empty((g, 128, n, 4), np.uint8)
        nib[..., 0::2] = words & 0xF
        nib[..., 1::2] = words >> 4
        vals = E2M1[nib]
    vals = vals * np.repeat(np.exp2(scales.astype(np.float64) - 127.0), 8, axis=1)[..., None]
    return vals.transpose(0, 1, 3, 2).reshape(g * 512, n)


K, T, J, I, N, M, L = 1024, 1024, 512, 512, 512, 512, 512


def setup_inputs():
    n = np.random.standard_normal
    idx = np.random.permutation(T)[:J]
    idx2 = np.random.permutation(T)[:I]
    fk = mx_kscale(K)
    fn = mx_kscale(N)
    fl = mx_kscale(L)
    xqp = pack_weight(n((K, T)) / fk[:, None], "e4m3")
    wap = pack_weight(n((K, N)) * 1 / np.sqrt(K) * fk[:, None] * fn, "e2m1")
    xip = pack_weight(n((L, I)) / fl[:, None], "e2m1")
    wip = pack_weight(n((L, M)) * 1 / np.sqrt(L) * fl[:, None], "e4m3")
    wmp = pack_weight(n((N, M)) * 1 / np.sqrt(N) / fn[:, None], "e2m1")
    return {
        "xq_words": xqp[0],
        "xq_scales": xqp[1],
        "wa_words": wap[0],
        "wa_scales": wap[1],
        "xi_words": xip[0],
        "xi_scales": xip[1],
        "wi_words": wip[0],
        "wi_scales": wip[1],
        "wm_words": wmp[0],
        "wm_scales": wmp[1],
        "offs": striped(idx),
        "offs2": striped(idx2),
    }


def reference(xq_words, xq_scales, wa_words, wa_scales, xi_words, xi_scales, wi_words, wi_scales, wm_words, wm_scales, offs, offs2):
    idx = unstriped(offs)
    idx2 = unstriped(offs2)
    xqu = unpack_weight(xq_words, xq_scales, "e4m3")
    wau = unpack_weight(wa_words, wa_scales, "e2m1")
    xiu = unpack_weight(xi_words, xi_scales, "e2m1")
    wiu = unpack_weight(wi_words, wi_scales, "e4m3")
    wmu = unpack_weight(wm_words, wm_scales, "e2m1")
    xqidxg = xqu[:, idx]
    p = wau.T @ xqidxg
    pr = np.maximum(p, 0.0)
    pg = np.zeros((N, T))
    pg[:, idx] = pr
    ms = pg[:, idx2]
    msq = mxq(ms, 0, "e4m3")
    y = wmu.T @ msq + wiu.T @ xiu
    return y

@@ -1,0 +1,213 @@
+from contextlib import ExitStack
+
+import concourse.mybir as mybir
+
+K, T, J, I, N, M, L = 1024, 1024, 512, 512, 512, 512, 512
+FLOPS = 2 * (K * N * J + N * M * I + L * M * I)
+
+F32 = mybir.dt.float32
+BF16 = mybir.dt.bfloat16
+I32 = mybir.dt.int32
+U32 = mybir.dt.uint32
+U16 = mybir.dt.uint16
+U8 = mybir.dt.uint8
+E4M3 = mybir.dt.float8_e4m3fn_x4
+E2M1 = mybir.dt.float4_e2m1fn_x4
+RELU = mybir.ActivationFunctionType.Relu
+
+P = 128
+PACK = 4
+QUADS = 4
+PASSES = K // (P * PACK)
+PER_COL = 16
+CHUNK = 128
+CHUNKS = I // CHUNK
+HALF = J // 2
+
+
+def load_scale_rows(queue, plane, rows):
+    for q in range(QUADS):
+        queue.dma_start(out=plane[32 * q : 32 * q + 4].bitcast(I32), in_=rows[4 * q : 4 * q + 4].bitcast(I32))
+
+
+def tile_list_expert_messages_kernel(
+    tc, xq_words, xq_scales, wa_words, wa_scales, xi_words, xi_scales, wi_words, wi_scales, wm_words, wm_scales, offs, offs2, out
+):
+    nc = tc.nc
+    with ExitStack() as ctx:
+        held = ctx.enter_context(tc.tile_pool(name="held", bufs=1))
+        ring = ctx.enter_context(tc.tile_pool(name="ring", bufs=2))
+        psum = ctx.enter_context(tc.psum_pool(name="psum", bufs=1))
+
+        list1 = held.tile([P, J // PER_COL], U16, name="list1")
+        list2 = held.tile([P, I // PER_COL], U16, name="list2")
+        nc.sync.dma_start(list1[:], offs)
+
+        xq_s = held.tile([P, T], U8, name="xq_s", align_bytes=64)
+        nc.gpsimd.memset(xq_s[:].bitcast(I32), 0)
+        wa_s_raw = held.tile([P, PASSES * N], U8, name="wa_s_raw", tag="planes", align_bytes=64)
+        nc.gpsimd.memset(wa_s_raw[:].bitcast(I32), 0)
+        for q in range(QUADS):
+            nc.sync.dma_start(out=xq_s[32 * q : 32 * q + 8, :].bitcast(I32), in_=xq_scales[:, 4 * q : 4 * q + 4, :].bitcast(I32))
+        wa_w_raw = held.tile([P, PASSES * 2 * N], U8, name="wa_w_raw", tag="words", align_bytes=64)
+        nc.sync.dma_start(
+            out=wa_w_raw[:].bitcast(I32).rearrange("p (z c) -> p z c", z=PASSES),
+            in_=wa_words.bitcast(I32).rearrange("z p c -> p z c"),
+        )
+        xq_w = []
+        for z in range(PASSES):
+            window = held.tile([P, T], I32, name="xq_w%d" % z, tag="wide%d" % z, align_bytes=64)
+            nc.sync.dma_start(out=window[:], in_=xq_words[z].rearrange("p n t -> p (n t)").bitcast(I32))
+            xq_w.append(window)
+        for q in range(QUADS):
+            nc.sync.dma_start(
+                out=wa_s_raw[32 * q : 32 * q + 4, :].bitcast(I32).rearrange("r (z c) -> r z c", z=PASSES),
+                in_=wa_scales[:, 4 * q : 4 * q + 4, :].bitcast(I32).rearrange("z r c -> r z c"),
+            )
+        nc.sync.dma_start(list2[:], offs2)
+
+        pages = []
+        for t in range(2):
+            page = held.tile([P, T], F32, name="page%d" % t, align_bytes=64)
+            nc.vector.memset(page[:], 0.0)
+            pages.append(page)
+
+        xg_s0 = held.tile([P, J], U8, name="xg_s0", align_bytes=64)
+        xg_s1 = held.tile([P, J], U8, name="xg_s1", align_bytes=64)
+        nc.gpsimd.memset(xg_s1[:].bitcast(I32), 0)
+        nc.vector.tensor_copy(xg_s0[:], xq_s[:].indirect(list1[:]))
+        for q in range(QUADS):
+            nc.scalar.dma_start(out=xg_s1[32 * q : 32 * q + 4, :].bitcast(I32), in_=xg_s0[32 * q + 4 : 32 * q + 8, :].bitcast(I32))
+        xg_s = [xg_s0, xg_s1]
+
+        wa_s = held.tile([P, PASSES, PACK, P], U8, name="wa_s", align_bytes=64)
+        wa_w = held.tile([P, PASSES * 2 * N], U8, name="wa_w", align_bytes=64)
+        nc.vector.tensor_copy(
+            wa_w[:].bitcast(U16).rearrange("p (z t c) -> p z t c", z=PASSES, t=PACK),
+            wa_w_raw[:].bitcast(U16).rearrange("p (z c t) -> p z t c", z=PASSES, t=PACK),
+        )
+
+        nc.vector.tensor_copy(wa_s[:], wa_s_raw[:].rearrange("p (z c t) -> p z t c", z=PASSES, t=PACK))
+
+        xg_w = []
+        for h in range(2):
+            xg_w.append(held.tile([P, PASSES, HALF], U32, name="xg_w%d" % h, tag=("first_half", "planes")[h], align_bytes=64))
+            for z in range(PASSES):
+                nc.vector.tensor_copy(
+                    xg_w[h][:, z, :],
+                    xq_w[z][:].bitcast(U32).indirect(list1[:, h * HALF // PER_COL : (h + 1) * HALF // PER_COL]),
+                )
+
+        for t in range(2, PACK):
+            page = held.tile([P, T], F32, name="page%d" % t, tag="wide%d" % (t - 2), align_bytes=64)
+            nc.gpsimd.memset(page[:], 0.0)
+            pages.append(page)
+
+        pieces = [(0, 0, HALF), (1, 0, HALF), (2, 0, J), (3, 0, J), (0, HALF, HALF), (1, HALF, HALF)]
+        for b, (t, first, width) in enumerate(pieces):
+            acc = psum.tile([P, width], F32, name="p_acc%d" % b, tag="bank%d" % (b % 2))
+            step = CHUNK
+            for z in range(PASSES):
+                col = (z * PACK + t) * P
+                for c0 in range(0, width, step):
+                    cols = slice(first + c0, first + c0 + step)
+                    nc.tensor.matmul_mx(
+                        out=acc[:, c0 : c0 + step],
+                        lhsT=wa_w[:, 2 * col : 2 * (col + P)].bitcast(E2M1),
+                        lhsT_scale=wa_s[:, z, t, :],
+                        rhs=xg_w[(first + c0) // HALF][:, z, (first + c0) % HALF : (first + c0) % HALF + step].bitcast(E4M3),
+                        rhs_scale=xg_s[z][:, cols],
+                        start=(z == 0 and c0 == 0),
+                        stop=(z == PASSES - 1 and c0 + step == width),
+                    )
+            pr = ring.tile([P, width], F32, name="pr%d" % b, tag="staged", align_bytes=64)
+            nc.scalar.activation(pr[:], acc[:], RELU)
+            nc.vector.tensor_copy(pages[t][:].indirect(list1[:, first // PER_COL : (first + width) // PER_COL]), pr[:])
+
+        late_s = held.tile([P, 3 * M], U8, name="late_s", tag="planes", align_bytes=64)
+        nc.gpsimd.memset(late_s[:].bitcast(I32), 0)
+        late_w = held.tile([P, 8 * M], U8, name="late_w", tag="words", align_bytes=64)
+        wi_w, xi_w, wm_w = late_w[:, 0 : 4 * M], late_w[:, 4 * M : 6 * M], late_w[:, 6 * M : 8 * M]
+        wi_s, xi_s, wm_s = late_s[:, 0:M], late_s[:, M : 2 * M], late_s[:, 2 * M : 3 * M]
+        nc.sync.dma_start(out=wi_w.bitcast(I32), in_=wi_words[0].rearrange("p n t -> p (n t)").bitcast(I32))
+        nc.sync.dma_start(out=xi_w.bitcast(I32), in_=xi_words[0].bitcast(I32))
+        nc.sync.dma_start(out=wm_w.bitcast(I32), in_=wm_words[0].bitcast(I32))
+        for plane, rows in ((wi_s, wi_scales), (xi_s, xi_scales), (wm_s, wm_scales)):
+            load_scale_rows(nc.sync, plane, rows[0])
+
+        slices = M // P
+        banks = [[(2, 0, slices)], [(3, 0, slices)], [(4, 0, slices)], [(5, 0, slices // 2), (6, slices // 2, slices // 2)]]
+        accs = []
+        for c in range(CHUNKS):
+            cols = slice(c * CHUNK, (c + 1) * CHUNK)
+            row = []
+            for b, m0, count in banks[c]:
+                acc = psum.tile([P, count, CHUNK], F32, name="y_acc%d_%d" % (c, m0), tag="bank%d" % b)
+                for m in range(m0, m0 + count):
+                    nc.tensor.matmul_mx(
+                        out=acc[:, m - m0, :],
+                        lhsT=wi_w[:, 4 * m * P : 4 * (m + 1) * P].bitcast(E4M3),
+                        lhsT_scale=wi_s[:, m * P : (m + 1) * P],
+                        rhs=xi_w[:, 2 * c * CHUNK : 2 * (c + 1) * CHUNK].bitcast(E2M1),
+                        rhs_scale=xi_s[:, cols],
+                        start=(m == m0),
+                        stop=False,
+                    )
+                row.append((acc, m0, count))
+            accs.append(row)
+
+        out_rows = out.rearrange("(m p) i -> p m i", p=P)
+        picked = {}
+        rounded = {}
+
+        def gather(c):
+            picked[c] = ring.tile([P, PACK, CHUNK], F32, name="picked%d" % c, tag="staged", align_bytes=64)
+            for t in (2, 3, 0, 1):
+                nc.vector.tensor_copy(
+                    picked[c][:, t, :], pages[t][:].indirect(list2[:, c * CHUNK // PER_COL : (c + 1) * CHUNK // PER_COL])
+                )
+
+        def weave(c):
+            rounded[c] = held.tile([P, CHUNK, PACK], BF16, name="rounded%d" % c, align_bytes=64)
+            source = picked[c][:].rearrange("p t i -> p i t")
+            if c == CHUNKS - 1:
+                nc.vector.tensor_copy(rounded[c][:], source)
+            else:
+                nc.scalar.copy(rounded[c][:], source)
+
+        def finish(c):
+            codes = held.tile([P, CHUNK], U32, name="codes%d" % c, align_bytes=64)
+            plane = held.tile([P, CHUNK], U8, name="plane%d" % c, align_bytes=64)
+            nc.vector.quantize_mx(out=codes[:].bitcast(E4M3), scales=plane[:], in_=rounded[c][:].rearrange("p i t -> p (i t)"))
+            for part, (acc, m0, count) in enumerate(accs[c]):
+                for m in range(m0, m0 + count):
+                    nc.tensor.matmul_mx(
+                        out=acc[:, m - m0, :],
+                        lhsT=wm_w[:, 2 * m * P : 2 * (m + 1) * P].bitcast(E2M1),
+                        lhsT_scale=wm_s[:, m * P : (m + 1) * P],
+                        rhs=codes[:].bitcast(E4M3),
+                        rhs_scale=plane[:],
+                        start=False,
+                        stop=(m == m0 + count - 1),
+                    )
+                result = held.tile([P, count, CHUNK], F32, name="result%d_%d" % (c, m0), align_bytes=64)
+                target = out_rows[:, m0 : m0 + count, c * CHUNK : (c + 1) * CHUNK]
+                if c == CHUNKS - 1 and part == 0:
+                    nc.scalar.copy(result[:], acc[:])
+                    nc.scalar.dma_start(out=target, in_=result[:])
+                elif c == CHUNKS - 1:
+                    nc.vector.tensor_copy(result[:], acc[:])
+                    nc.sync.dma_start(out=target, in_=result[:])
+                else:
+                    nc.scalar.copy(result[:], acc[:])
+                    nc.sync.dma_start(out=target, in_=result[:])
+
+        gather(0)
+        weave(0)
+        for c in range(1, CHUNKS):
+            gather(c)
+            if c < CHUNKS - 1:
+                weave(c)
+            finish(c - 1)
+        weave(CHUNKS - 1)
+        finish(CHUNKS - 1)

@@ -43,12 +43,13 @@ def tile_list_expert_messages_kernel(
         list2 = held.tile([P, I // PER_COL], U16, name="list2")
         nc.sync.dma_start(list1[:], offs)
 
-        xq_s = held.tile([P, T], U8, name="xq_s", align_bytes=64)
+        xq_s = held.tile([P, T], U8, name="xq_s", tag="early", align_bytes=64)
         nc.gpsimd.memset(xq_s[:].bitcast(I32), 0)
         wa_s_raw = held.tile([P, PASSES * N], U8, name="wa_s_raw", tag="planes", align_bytes=64)
         nc.gpsimd.memset(wa_s_raw[:].bitcast(I32), 0)
         for q in range(QUADS):
-            nc.sync.dma_start(out=xq_s[32 * q : 32 * q + 8, :].bitcast(I32), in_=xq_scales[:, 4 * q : 4 * q + 4, :].bitcast(I32))
+            nc.scalar.dma_start(out=xq_s[32 * q : 32 * q + 8, :].bitcast(I32), in_=xq_scales[:, 4 * q : 4 * q + 4, :].bitcast(I32))
+        nc.sync.dma_start(list2[:], offs2)
         wa_w_raw = held.tile([P, PASSES * 2 * N], U8, name="wa_w_raw", tag="words", align_bytes=64)
         nc.sync.dma_start(
             out=wa_w_raw[:].bitcast(I32).rearrange("p (z c) -> p z c", z=PASSES),
@@ -64,12 +65,11 @@ def tile_list_expert_messages_kernel(
                 out=wa_s_raw[32 * q : 32 * q + 4, :].bitcast(I32).rearrange("r (z c) -> r z c", z=PASSES),
                 in_=wa_scales[:, 4 * q : 4 * q + 4, :].bitcast(I32).rearrange("z r c -> r z c"),
             )
-        nc.sync.dma_start(list2[:], offs2)
 
         pages = []
-        for t in range(2):
+        for t in range(PACK):
             page = held.tile([P, T], F32, name="page%d" % t, align_bytes=64)
-            nc.vector.memset(page[:], 0.0)
+            nc.vector.memset(page[:].bitcast(I32), 0)
             pages.append(page)
 
         xg_s0 = held.tile([P, J], U8, name="xg_s0", align_bytes=64)
@@ -80,28 +80,28 @@ def tile_list_expert_messages_kernel(
             nc.scalar.dma_start(out=xg_s1[32 * q : 32 * q + 4, :].bitcast(I32), in_=xg_s0[32 * q + 4 : 32 * q + 8, :].bitcast(I32))
         xg_s = [xg_s0, xg_s1]
 
-        wa_s = held.tile([P, PASSES, PACK, P], U8, name="wa_s", align_bytes=64)
         wa_w = held.tile([P, PASSES * 2 * N], U8, name="wa_w", align_bytes=64)
         nc.vector.tensor_copy(
             wa_w[:].bitcast(U16).rearrange("p (z t c) -> p z t c", z=PASSES, t=PACK),
             wa_w_raw[:].bitcast(U16).rearrange("p (z c t) -> p z t c", z=PASSES, t=PACK),
         )
 
-        nc.vector.tensor_copy(wa_s[:], wa_s_raw[:].rearrange("p (z c t) -> p z t c", z=PASSES, t=PACK))
 
-        xg_w = []
-        for h in range(2):
-            xg_w.append(held.tile([P, PASSES, HALF], U32, name="xg_w%d" % h, tag=("first_half", "planes")[h], align_bytes=64))
-            for z in range(PASSES):
-                nc.vector.tensor_copy(
-                    xg_w[h][:, z, :],
-                    xq_w[z][:].bitcast(U32).indirect(list1[:, h * HALF // PER_COL : (h + 1) * HALF // PER_COL]),
-                )
+        early = held.tile([P, J + HALF], U32, name="early", tag="early", align_bytes=64)
+        nc.vector.tensor_copy(early[:, 0:J], xq_w[0][:].bitcast(U32).indirect(list1[:]))
+        nc.vector.tensor_copy(early[:, J : J + HALF], xq_w[1][:].bitcast(U32).indirect(list1[:, 0 : HALF // PER_COL]))
+        by_slice = wa_s_raw[:].rearrange("p (z c t) -> p z t c", z=PASSES, t=PACK)
+        wa_s_first = held.tile([P, PASSES, 1, P], U8, name="wa_s_first", align_bytes=64)
+        nc.vector.tensor_copy(wa_s_first[:], by_slice[:, :, 0:1, :])
+        wa_s_rest = held.tile([P, PASSES, PACK - 1, P], U8, name="wa_s_rest", align_bytes=64)
+        nc.vector.tensor_copy(wa_s_rest[:], by_slice[:, :, 1:PACK, :])
+        later = held.tile([P, HALF], U32, name="later", tag="planes", align_bytes=64)
+        nc.vector.tensor_copy(later[:], xq_w[1][:].bitcast(U32).indirect(list1[:, HALF // PER_COL : J // PER_COL]))
 
-        for t in range(2, PACK):
-            page = held.tile([P, T], F32, name="page%d" % t, tag="wide%d" % (t - 2), align_bytes=64)
-            nc.gpsimd.memset(page[:], 0.0)
-            pages.append(page)
+        def picked_words(z, j0):
+            if z == 1 and j0 >= HALF:
+                return later[:, j0 - HALF : j0 - HALF + CHUNK]
+            return early[:, z * J + j0 : z * J + j0 + CHUNK]
 
         pieces = [(0, 0, HALF), (1, 0, HALF), (2, 0, J), (3, 0, J), (0, HALF, HALF), (1, HALF, HALF)]
         for b, (t, first, width) in enumerate(pieces):
@@ -114,8 +114,8 @@ def tile_list_expert_messages_kernel(
                     nc.tensor.matmul_mx(
                         out=acc[:, c0 : c0 + step],
                         lhsT=wa_w[:, 2 * col : 2 * (col + P)].bitcast(E2M1),
-                        lhsT_scale=wa_s[:, z, t, :],
-                        rhs=xg_w[(first + c0) // HALF][:, z, (first + c0) % HALF : (first + c0) % HALF + step].bitcast(E4M3),
+                        lhsT_scale=wa_s_first[:, z, 0, :] if t == 0 else wa_s_rest[:, z, t - 1, :],
+                        rhs=picked_words(z, first + c0).bitcast(E4M3),
                         rhs_scale=xg_s[z][:, cols],
                         start=(z == 0 and c0 == 0),
                         stop=(z == PASSES - 1 and c0 + step == width),
@@ -157,57 +157,63 @@ def tile_list_expert_messages_kernel(
             accs.append(row)
 
         out_rows = out.rearrange("(m p) i -> p m i", p=P)
+        groups = [(0, 2), (2, 1), (3, 1)]
+        last = len(groups) - 1
         picked = {}
         rounded = {}
 
-        def gather(c):
-            picked[c] = ring.tile([P, PACK, CHUNK], F32, name="picked%d" % c, tag="staged", align_bytes=64)
+        def gather(g):
+            c0, n = groups[g]
+            picked[g] = ring.tile([P, PACK, n * CHUNK], F32, name="picked%d" % g, tag="staged", align_bytes=64)
             for t in (2, 3, 0, 1):
                 nc.vector.tensor_copy(
-                    picked[c][:, t, :], pages[t][:].indirect(list2[:, c * CHUNK // PER_COL : (c + 1) * CHUNK // PER_COL])
+                    picked[g][:, t, :], pages[t][:].indirect(list2[:, c0 * CHUNK // PER_COL : (c0 + n) * CHUNK // PER_COL])
                 )
 
-        def weave(c):
-            rounded[c] = held.tile([P, CHUNK, PACK], BF16, name="rounded%d" % c, align_bytes=64)
-            source = picked[c][:].rearrange("p t i -> p i t")
-            if c == CHUNKS - 1:
-                nc.vector.tensor_copy(rounded[c][:], source)
+        def weave(g):
+            rounded[g] = held.tile([P, groups[g][1] * CHUNK, PACK], BF16, name="rounded%d" % g, align_bytes=64)
+            source = picked[g][:].rearrange("p t i -> p i t")
+            if g == last:
+                nc.vector.tensor_copy(rounded[g][:], source)
             else:
-                nc.scalar.copy(rounded[c][:], source)
+                nc.scalar.copy(rounded[g][:], source)
 
-        def finish(c):
-            codes = held.tile([P, CHUNK], U32, name="codes%d" % c, align_bytes=64)
-            plane = held.tile([P, CHUNK], U8, name="plane%d" % c, align_bytes=64)
-            nc.vector.quantize_mx(out=codes[:].bitcast(E4M3), scales=plane[:], in_=rounded[c][:].rearrange("p i t -> p (i t)"))
-            for part, (acc, m0, count) in enumerate(accs[c]):
-                for m in range(m0, m0 + count):
-                    nc.tensor.matmul_mx(
-                        out=acc[:, m - m0, :],
-                        lhsT=wm_w[:, 2 * m * P : 2 * (m + 1) * P].bitcast(E2M1),
-                        lhsT_scale=wm_s[:, m * P : (m + 1) * P],
-                        rhs=codes[:].bitcast(E4M3),
-                        rhs_scale=plane[:],
-                        start=False,
-                        stop=(m == m0 + count - 1),
-                    )
-                result = held.tile([P, count, CHUNK], F32, name="result%d_%d" % (c, m0), align_bytes=64)
-                target = out_rows[:, m0 : m0 + count, c * CHUNK : (c + 1) * CHUNK]
-                if c == CHUNKS - 1 and part == 0:
-                    nc.scalar.copy(result[:], acc[:])
-                    nc.scalar.dma_start(out=target, in_=result[:])
-                elif c == CHUNKS - 1:
-                    nc.vector.tensor_copy(result[:], acc[:])
-                    nc.sync.dma_start(out=target, in_=result[:])
-                else:
-                    nc.scalar.copy(result[:], acc[:])
-                    nc.sync.dma_start(out=target, in_=result[:])
+        def finish(g):
+            c0, n = groups[g]
+            codes = held.tile([P, n * CHUNK], U32, name="codes%d" % g, align_bytes=64)
+            plane = held.tile([P, n * CHUNK], U8, name="plane%d" % g, align_bytes=64)
+            nc.vector.quantize_mx(out=codes[:].bitcast(E4M3), scales=plane[:], in_=rounded[g][:].rearrange("p i t -> p (i t)"))
+            for c in range(c0, c0 + n):
+                cols = slice((c - c0) * CHUNK, (c - c0 + 1) * CHUNK)
+                for part, (acc, m0, count) in enumerate(accs[c]):
+                    for m in range(m0, m0 + count):
+                        nc.tensor.matmul_mx(
+                            out=acc[:, m - m0, :],
+                            lhsT=wm_w[:, 2 * m * P : 2 * (m + 1) * P].bitcast(E2M1),
+                            lhsT_scale=wm_s[:, m * P : (m + 1) * P],
+                            rhs=codes[:, cols].bitcast(E4M3),
+                            rhs_scale=plane[:, cols],
+                            start=False,
+                            stop=(m == m0 + count - 1),
+                        )
+                    result = held.tile([P, count, CHUNK], F32, name="result%d_%d" % (c, m0), align_bytes=64)
+                    target = out_rows[:, m0 : m0 + count, c * CHUNK : (c + 1) * CHUNK]
+                    if g == last and part == 0:
+                        nc.scalar.copy(result[:], acc[:])
+                        nc.scalar.dma_start(out=target, in_=result[:])
+                    elif g == last:
+                        nc.vector.tensor_copy(result[:], acc[:])
+                        nc.sync.dma_start(out=target, in_=result[:])
+                    else:
+                        nc.scalar.copy(result[:], acc[:])
+                        nc.sync.dma_start(out=target, in_=result[:])
 
         gather(0)
         weave(0)
-        for c in range(1, CHUNKS):
-            gather(c)
-            if c < CHUNKS - 1:
-                weave(c)
-            finish(c - 1)
-        weave(CHUNKS - 1)
-        finish(CHUNKS - 1)
+        for g in range(1, last + 1):
+            gather(g)
+            if g < last:
+                weave(g)
+            finish(g - 1)
+        weave(last)
+        finish(last)

@@ -22,7 +22,7 @@ PASSES = K // (P * PACK)
 PER_COL = 16
 CHUNK = 128
 CHUNKS = I // CHUNK
-HALF = J // 2
+HALF = 128
 
 
 def load_scale_rows(queue, plane, rows):
@@ -43,14 +43,14 @@ def tile_list_expert_messages_kernel(
         list2 = held.tile([P, I // PER_COL], U16, name="list2")
         nc.sync.dma_start(list1[:], offs)
 
-        xq_s = held.tile([P, T], U8, name="xq_s", tag="early", align_bytes=64)
+        xq_s = held.tile([P, T], U8, name="xq_s", align_bytes=64)
         nc.gpsimd.memset(xq_s[:].bitcast(I32), 0)
         wa_s_raw = held.tile([P, PASSES * N], U8, name="wa_s_raw", tag="planes", align_bytes=64)
         nc.gpsimd.memset(wa_s_raw[:].bitcast(I32), 0)
         for q in range(QUADS):
-            nc.scalar.dma_start(out=xq_s[32 * q : 32 * q + 8, :].bitcast(I32), in_=xq_scales[:, 4 * q : 4 * q + 4, :].bitcast(I32))
+            nc.sync.dma_start(out=xq_s[32 * q : 32 * q + 8, :].bitcast(I32), in_=xq_scales[:, 4 * q : 4 * q + 4, :].bitcast(I32))
         nc.sync.dma_start(list2[:], offs2)
-        wa_w_raw = held.tile([P, PASSES * 2 * N], U8, name="wa_w_raw", tag="words", align_bytes=64)
+        wa_w_raw = held.tile([P, PASSES * 2 * N], U8, name="wa_w_raw", align_bytes=64)
         nc.sync.dma_start(
             out=wa_w_raw[:].bitcast(I32).rearrange("p (z c) -> p z c", z=PASSES),
             in_=wa_words.bitcast(I32).rearrange("z p c -> p z c"),
@@ -76,8 +76,8 @@ def tile_list_expert_messages_kernel(
         xg_s1 = held.tile([P, J], U8, name="xg_s1", align_bytes=64)
         nc.gpsimd.memset(xg_s1[:].bitcast(I32), 0)
         nc.vector.tensor_copy(xg_s0[:], xq_s[:].indirect(list1[:]))
-        for q in range(QUADS):
-            nc.scalar.dma_start(out=xg_s1[32 * q : 32 * q + 4, :].bitcast(I32), in_=xg_s0[32 * q + 4 : 32 * q + 8, :].bitcast(I32))
+        for first, rows in ((0, 64), (64, 4), (96, 4)):
+            nc.sync.dma_start(out=xg_s1[first : first + rows, :].bitcast(I32), in_=xg_s0[first + 4 : first + 4 + rows, :].bitcast(I32))
         xg_s = [xg_s0, xg_s1]
 
         wa_w = held.tile([P, PASSES * 2 * N], U8, name="wa_w", align_bytes=64)
@@ -87,7 +87,7 @@ def tile_list_expert_messages_kernel(
         )
 
 
-        early = held.tile([P, J + HALF], U32, name="early", tag="early", align_bytes=64)
+        early = held.tile([P, J + HALF], U32, name="early", align_bytes=64)
         nc.vector.tensor_copy(early[:, 0:J], xq_w[0][:].bitcast(U32).indirect(list1[:]))
         nc.vector.tensor_copy(early[:, J : J + HALF], xq_w[1][:].bitcast(U32).indirect(list1[:, 0 : HALF // PER_COL]))
         by_slice = wa_s_raw[:].rearrange("p (z c t) -> p z t c", z=PASSES, t=PACK)
@@ -95,7 +95,7 @@ def tile_list_expert_messages_kernel(
         nc.vector.tensor_copy(wa_s_first[:], by_slice[:, :, 0:1, :])
         wa_s_rest = held.tile([P, PASSES, PACK - 1, P], U8, name="wa_s_rest", align_bytes=64)
         nc.vector.tensor_copy(wa_s_rest[:], by_slice[:, :, 1:PACK, :])
-        later = held.tile([P, HALF], U32, name="later", tag="planes", align_bytes=64)
+        later = held.tile([P, J - HALF], U32, name="later", tag="planes", align_bytes=64)
         nc.vector.tensor_copy(later[:], xq_w[1][:].bitcast(U32).indirect(list1[:, HALF // PER_COL : J // PER_COL]))
 
         def picked_words(z, j0):
@@ -103,7 +103,7 @@ def tile_list_expert_messages_kernel(
                 return later[:, j0 - HALF : j0 - HALF + CHUNK]
             return early[:, z * J + j0 : z * J + j0 + CHUNK]
 
-        pieces = [(0, 0, HALF), (1, 0, HALF), (2, 0, J), (3, 0, J), (0, HALF, HALF), (1, HALF, HALF)]
+        pieces = [(0, 0, HALF), (1, 0, HALF), (0, HALF, J - HALF), (1, HALF, J - HALF), (2, 0, J), (3, 0, J)]
         for b, (t, first, width) in enumerate(pieces):
             acc = psum.tile([P, width], F32, name="p_acc%d" % b, tag="bank%d" % (b % 2))
             step = CHUNK
@@ -126,7 +126,7 @@ def tile_list_expert_messages_kernel(
 
         late_s = held.tile([P, 3 * M], U8, name="late_s", tag="planes", align_bytes=64)
         nc.gpsimd.memset(late_s[:].bitcast(I32), 0)
-        late_w = held.tile([P, 8 * M], U8, name="late_w", tag="words", align_bytes=64)
+        late_w = held.tile([P, 8 * M], U8, name="late_w", tag="wide0", align_bytes=64)
         wi_w, xi_w, wm_w = late_w[:, 0 : 4 * M], late_w[:, 4 * M : 6 * M], late_w[:, 6 * M : 8 * M]
         wi_s, xi_s, wm_s = late_s[:, 0:M], late_s[:, M : 2 * M], late_s[:, 2 * M : 3 * M]
         nc.sync.dma_start(out=wi_w.bitcast(I32), in_=wi_words[0].rearrange("p n t -> p (n t)").bitcast(I32))
@@ -136,7 +136,7 @@ def tile_list_expert_messages_kernel(
             load_scale_rows(nc.sync, plane, rows[0])
 
         slices = M // P
-        banks = [[(2, 0, slices)], [(3, 0, slices)], [(4, 0, slices)], [(5, 0, slices // 2), (6, slices // 2, slices // 2)]]
+        banks = [[(2, 0, slices)], [(3, 0, slices)], [(4, 0, slices)], [(5, 0, 2), (6, 2, 1), (7, 3, 1)]]
         accs = []
         for c in range(CHUNKS):
             cols = slice(c * CHUNK, (c + 1) * CHUNK)
@@ -165,7 +165,7 @@ def tile_list_expert_messages_kernel(
         def gather(g):
             c0, n = groups[g]
             picked[g] = ring.tile([P, PACK, n * CHUNK], F32, name="picked%d" % g, tag="staged", align_bytes=64)
-            for t in (2, 3, 0, 1):
+            for t in range(PACK):
                 nc.vector.tensor_copy(
                     picked[g][:, t, :], pages[t][:].indirect(list2[:, c0 * CHUNK // PER_COL : (c0 + n) * CHUNK // PER_COL])
                 )

@@ -17,38 +17,47 @@ RELU = mybir.ActivationFunctionType.Relu
 
 P = 128
 PACK = 4
-QUADS = 4
 PASSES = K // (P * PACK)
-PER_COL = 16
-CHUNK = 128
-CHUNKS = I // CHUNK
-HALF = 128
+QUADRANT = 32
+LIVE = 4
+PER_COLUMN = 16
+WIDTH = 128
+LEAD = WIDTH
+STAGE1_BANKS = 2
+STAGED = 2
+
+PIECES = [(t, 0, LEAD) for t in range(PACK - 1)] + [(t, LEAD, J - LEAD) for t in range(PACK - 1)] + [(PACK - 1, 0, J)]
+
+GROUPS = [(0, 2 * WIDTH, [(0, 2), (2, 2)]), (2 * WIDTH, WIDTH, [(0, 4)]), (3 * WIDTH, WIDTH, [(0, 2), (2, 1), (3, 1)])]
 
 
-def load_scale_rows(queue, plane, rows):
-    for q in range(QUADS):
-        queue.dma_start(out=plane[32 * q : 32 * q + 4].bitcast(I32), in_=rows[4 * q : 4 * q + 4].bitcast(I32))
+def entries(offsets, first, count):
+    return offsets[:, first // PER_COLUMN : (first + count) // PER_COLUMN]
 
 
 def tile_list_expert_messages_kernel(
     tc, xq_words, xq_scales, wa_words, wa_scales, xi_words, xi_scales, wi_words, wi_scales, wm_words, wm_scales, offs, offs2, out
 ):
     nc = tc.nc
+    quadrants = range(P // QUADRANT)
     with ExitStack() as ctx:
         held = ctx.enter_context(tc.tile_pool(name="held", bufs=1))
-        ring = ctx.enter_context(tc.tile_pool(name="ring", bufs=2))
+        ring = ctx.enter_context(tc.tile_pool(name="ring", bufs=STAGED))
         psum = ctx.enter_context(tc.psum_pool(name="psum", bufs=1))
 
-        list1 = held.tile([P, J // PER_COL], U16, name="list1")
-        list2 = held.tile([P, I // PER_COL], U16, name="list2")
+        list1 = held.tile([P, J // PER_COLUMN], U16, name="list1")
+        list2 = held.tile([P, I // PER_COLUMN], U16, name="list2")
         nc.sync.dma_start(list1[:], offs)
 
         xq_s = held.tile([P, T], U8, name="xq_s", align_bytes=64)
         nc.gpsimd.memset(xq_s[:].bitcast(I32), 0)
-        wa_s_raw = held.tile([P, PASSES * N], U8, name="wa_s_raw", tag="planes", align_bytes=64)
+        wa_s_raw = held.tile([P, PASSES * N], U8, name="wa_s_raw", tag="narrow", align_bytes=64)
         nc.gpsimd.memset(wa_s_raw[:].bitcast(I32), 0)
-        for q in range(QUADS):
-            nc.sync.dma_start(out=xq_s[32 * q : 32 * q + 8, :].bitcast(I32), in_=xq_scales[:, 4 * q : 4 * q + 4, :].bitcast(I32))
+        for g in quadrants:
+            nc.sync.dma_start(
+                out=xq_s[QUADRANT * g : QUADRANT * g + PASSES * LIVE, :].bitcast(I32),
+                in_=xq_scales[:, LIVE * g : LIVE * (g + 1), :].bitcast(I32),
+            )
         nc.sync.dma_start(list2[:], offs2)
         wa_w_raw = held.tile([P, PASSES * 2 * N], U8, name="wa_w_raw", align_bytes=64)
         nc.sync.dma_start(
@@ -60,10 +69,10 @@ def tile_list_expert_messages_kernel(
             window = held.tile([P, T], I32, name="xq_w%d" % z, tag="wide%d" % z, align_bytes=64)
             nc.sync.dma_start(out=window[:], in_=xq_words[z].rearrange("p n t -> p (n t)").bitcast(I32))
             xq_w.append(window)
-        for q in range(QUADS):
+        for g in quadrants:
             nc.sync.dma_start(
-                out=wa_s_raw[32 * q : 32 * q + 4, :].bitcast(I32).rearrange("r (z c) -> r z c", z=PASSES),
-                in_=wa_scales[:, 4 * q : 4 * q + 4, :].bitcast(I32).rearrange("z r c -> r z c"),
+                out=wa_s_raw[QUADRANT * g : QUADRANT * g + LIVE, :].bitcast(I32).rearrange("r (z c) -> r z c", z=PASSES),
+                in_=wa_scales[:, LIVE * g : LIVE * (g + 1), :].bitcast(I32).rearrange("z r c -> r z c"),
             )
 
         pages = []
@@ -74,10 +83,11 @@ def tile_list_expert_messages_kernel(
 
         xg_s0 = held.tile([P, J], U8, name="xg_s0", align_bytes=64)
         xg_s1 = held.tile([P, J], U8, name="xg_s1", align_bytes=64)
-        nc.gpsimd.memset(xg_s1[:].bitcast(I32), 0)
         nc.vector.tensor_copy(xg_s0[:], xq_s[:].indirect(list1[:]))
-        for first, rows in ((0, 64), (64, 4), (96, 4)):
-            nc.sync.dma_start(out=xg_s1[first : first + rows, :].bitcast(I32), in_=xg_s0[first + 4 : first + 4 + rows, :].bitcast(I32))
+        for first, rows in ((0, 2 * QUADRANT), (2 * QUADRANT, LIVE), (3 * QUADRANT, LIVE)):
+            nc.sync.dma_start(
+                out=xg_s1[first : first + rows, :].bitcast(I32), in_=xg_s0[first + LIVE : first + LIVE + rows, :].bitcast(I32)
+            )
         xg_s = [xg_s0, xg_s1]
 
         wa_w = held.tile([P, PASSES * 2 * N], U8, name="wa_w", align_bytes=64)
@@ -86,134 +96,128 @@ def tile_list_expert_messages_kernel(
             wa_w_raw[:].bitcast(U16).rearrange("p (z c t) -> p z t c", z=PASSES, t=PACK),
         )
 
-
-        early = held.tile([P, J + HALF], U32, name="early", align_bytes=64)
-        nc.vector.tensor_copy(early[:, 0:J], xq_w[0][:].bitcast(U32).indirect(list1[:]))
-        nc.vector.tensor_copy(early[:, J : J + HALF], xq_w[1][:].bitcast(U32).indirect(list1[:, 0 : HALF // PER_COL]))
+        xg_lead = held.tile([P, J + LEAD], U32, name="xg_lead", align_bytes=64)
+        nc.vector.tensor_copy(xg_lead[:, 0:J], xq_w[0][:].bitcast(U32).indirect(list1[:]))
+        nc.vector.tensor_copy(xg_lead[:, J : J + LEAD], xq_w[1][:].bitcast(U32).indirect(entries(list1, 0, LEAD)))
         by_slice = wa_s_raw[:].rearrange("p (z c t) -> p z t c", z=PASSES, t=PACK)
         wa_s_first = held.tile([P, PASSES, 1, P], U8, name="wa_s_first", align_bytes=64)
         nc.vector.tensor_copy(wa_s_first[:], by_slice[:, :, 0:1, :])
         wa_s_rest = held.tile([P, PASSES, PACK - 1, P], U8, name="wa_s_rest", align_bytes=64)
         nc.vector.tensor_copy(wa_s_rest[:], by_slice[:, :, 1:PACK, :])
-        later = held.tile([P, J - HALF], U32, name="later", tag="planes", align_bytes=64)
-        nc.vector.tensor_copy(later[:], xq_w[1][:].bitcast(U32).indirect(list1[:, HALF // PER_COL : J // PER_COL]))
+        xg_rest = held.tile([P, J - LEAD], U32, name="xg_rest", tag="narrow", align_bytes=64)
+        nc.vector.tensor_copy(xg_rest[:], xq_w[1][:].bitcast(U32).indirect(entries(list1, LEAD, J - LEAD)))
 
-        def picked_words(z, j0):
-            if z == 1 and j0 >= HALF:
-                return later[:, j0 - HALF : j0 - HALF + CHUNK]
-            return early[:, z * J + j0 : z * J + j0 + CHUNK]
+        def xg_words(z, j0):
+            if z == 1 and j0 >= LEAD:
+                return xg_rest[:, j0 - LEAD : j0 - LEAD + WIDTH]
+            return xg_lead[:, z * J + j0 : z * J + j0 + WIDTH]
 
-        pieces = [(0, 0, HALF), (1, 0, HALF), (0, HALF, J - HALF), (1, HALF, J - HALF), (2, 0, J), (3, 0, J)]
-        for b, (t, first, width) in enumerate(pieces):
-            acc = psum.tile([P, width], F32, name="p_acc%d" % b, tag="bank%d" % (b % 2))
-            step = CHUNK
+        for b, (t, first, count) in enumerate(PIECES):
+            acc = psum.tile([P, count], F32, name="p_acc%d" % b, tag="bank%d" % (b % STAGE1_BANKS))
             for z in range(PASSES):
-                col = (z * PACK + t) * P
-                for c0 in range(0, width, step):
-                    cols = slice(first + c0, first + c0 + step)
+                column = (z * PACK + t) * P
+                for c0 in range(0, count, WIDTH):
                     nc.tensor.matmul_mx(
-                        out=acc[:, c0 : c0 + step],
-                        lhsT=wa_w[:, 2 * col : 2 * (col + P)].bitcast(E2M1),
+                        out=acc[:, c0 : c0 + WIDTH],
+                        lhsT=wa_w[:, 2 * column : 2 * (column + P)].bitcast(E2M1),
                         lhsT_scale=wa_s_first[:, z, 0, :] if t == 0 else wa_s_rest[:, z, t - 1, :],
-                        rhs=picked_words(z, first + c0).bitcast(E4M3),
-                        rhs_scale=xg_s[z][:, cols],
+                        rhs=xg_words(z, first + c0).bitcast(E4M3),
+                        rhs_scale=xg_s[z][:, first + c0 : first + c0 + WIDTH],
                         start=(z == 0 and c0 == 0),
-                        stop=(z == PASSES - 1 and c0 + step == width),
+                        stop=(z == PASSES - 1 and c0 + WIDTH == count),
                     )
-            pr = ring.tile([P, width], F32, name="pr%d" % b, tag="staged", align_bytes=64)
+            if b < len(PIECES) - STAGED:
+                pr = held.tile([P, count], F32, name="pr%d" % b, align_bytes=64)
+            else:
+                pr = ring.tile([P, count], F32, name="pr%d" % b, tag="staged", align_bytes=64)
             nc.scalar.activation(pr[:], acc[:], RELU)
-            nc.vector.tensor_copy(pages[t][:].indirect(list1[:, first // PER_COL : (first + width) // PER_COL]), pr[:])
+            nc.vector.tensor_copy(pages[t][:].indirect(entries(list1, first, count)), pr[:])
 
-        late_s = held.tile([P, 3 * M], U8, name="late_s", tag="planes", align_bytes=64)
-        nc.gpsimd.memset(late_s[:].bitcast(I32), 0)
-        late_w = held.tile([P, 8 * M], U8, name="late_w", tag="wide0", align_bytes=64)
-        wi_w, xi_w, wm_w = late_w[:, 0 : 4 * M], late_w[:, 4 * M : 6 * M], late_w[:, 6 * M : 8 * M]
-        wi_s, xi_s, wm_s = late_s[:, 0:M], late_s[:, M : 2 * M], late_s[:, 2 * M : 3 * M]
+        late_s = held.tile([P, M + I + M], U8, name="late_s", tag="narrow", align_bytes=64)
+        late_w = held.tile([P, 4 * M + 2 * I + 2 * M], U8, name="late_w", tag="wide0", align_bytes=64)
+        wi_w, xi_w, wm_w = late_w[:, 0 : 4 * M], late_w[:, 4 * M : 4 * M + 2 * I], late_w[:, 4 * M + 2 * I : 6 * M + 2 * I]
+        wi_s, xi_s, wm_s = late_s[:, 0:M], late_s[:, M : M + I], late_s[:, M + I : 2 * M + I]
         nc.sync.dma_start(out=wi_w.bitcast(I32), in_=wi_words[0].rearrange("p n t -> p (n t)").bitcast(I32))
         nc.sync.dma_start(out=xi_w.bitcast(I32), in_=xi_words[0].bitcast(I32))
         nc.sync.dma_start(out=wm_w.bitcast(I32), in_=wm_words[0].bitcast(I32))
-        for plane, rows in ((wi_s, wi_scales), (xi_s, xi_scales), (wm_s, wm_scales)):
-            load_scale_rows(nc.sync, plane, rows[0])
+        for plane, rows in ((wi_s, wi_scales[0]), (xi_s, xi_scales[0]), (wm_s, wm_scales[0])):
+            for g in quadrants:
+                nc.sync.dma_start(
+                    out=plane[QUADRANT * g : QUADRANT * g + LIVE].bitcast(I32), in_=rows[LIVE * g : LIVE * (g + 1)].bitcast(I32)
+                )
 
-        slices = M // P
-        banks = [[(2, 0, slices)], [(3, 0, slices)], [(4, 0, slices)], [(5, 0, 2), (6, 2, 1), (7, 3, 1)]]
-        accs = []
-        for c in range(CHUNKS):
-            cols = slice(c * CHUNK, (c + 1) * CHUNK)
-            row = []
-            for b, m0, count in banks[c]:
-                acc = psum.tile([P, count, CHUNK], F32, name="y_acc%d_%d" % (c, m0), tag="bank%d" % b)
-                for m in range(m0, m0 + count):
-                    nc.tensor.matmul_mx(
-                        out=acc[:, m - m0, :],
-                        lhsT=wi_w[:, 4 * m * P : 4 * (m + 1) * P].bitcast(E4M3),
-                        lhsT_scale=wi_s[:, m * P : (m + 1) * P],
-                        rhs=xi_w[:, 2 * c * CHUNK : 2 * (c + 1) * CHUNK].bitcast(E2M1),
-                        rhs_scale=xi_s[:, cols],
-                        start=(m == m0),
-                        stop=False,
-                    )
-                row.append((acc, m0, count))
-            accs.append(row)
+        sums = {}
+        for group, (i0, columns, parts) in enumerate(GROUPS):
+            for m0, blocks in parts:
+                bank = STAGE1_BANKS + len(sums)
+                acc = psum.tile([P, blocks, columns], F32, name="y_acc%d" % bank, tag="bank%d" % bank)
+                sums[(group, m0)] = acc
+                for m in range(m0, m0 + blocks):
+                    for c0 in range(0, columns, WIDTH):
+                        nc.tensor.matmul_mx(
+                            out=acc[:, m - m0, c0 : c0 + WIDTH],
+                            lhsT=wi_w[:, 4 * m * P : 4 * (m + 1) * P].bitcast(E4M3),
+                            lhsT_scale=wi_s[:, m * P : (m + 1) * P],
+                            rhs=xi_w[:, 2 * (i0 + c0) : 2 * (i0 + c0 + WIDTH)].bitcast(E2M1),
+                            rhs_scale=xi_s[:, i0 + c0 : i0 + c0 + WIDTH],
+                            start=(m == m0 and c0 == 0),
+                            stop=False,
+                        )
 
         out_rows = out.rearrange("(m p) i -> p m i", p=P)
-        groups = [(0, 2), (2, 1), (3, 1)]
-        last = len(groups) - 1
+        last = len(GROUPS) - 1
         picked = {}
         rounded = {}
 
-        def gather(g):
-            c0, n = groups[g]
-            picked[g] = ring.tile([P, PACK, n * CHUNK], F32, name="picked%d" % g, tag="staged", align_bytes=64)
+        def gather(group):
+            i0, columns, parts = GROUPS[group]
+            picked[group] = ring.tile([P, PACK, columns], F32, name="picked%d" % group, tag="staged", align_bytes=64)
             for t in range(PACK):
-                nc.vector.tensor_copy(
-                    picked[g][:, t, :], pages[t][:].indirect(list2[:, c0 * CHUNK // PER_COL : (c0 + n) * CHUNK // PER_COL])
-                )
+                nc.vector.tensor_copy(picked[group][:, t, :], pages[t][:].indirect(entries(list2, i0, columns)))
 
-        def weave(g):
-            rounded[g] = held.tile([P, groups[g][1] * CHUNK, PACK], BF16, name="rounded%d" % g, align_bytes=64)
-            source = picked[g][:].rearrange("p t i -> p i t")
-            if g == last:
-                nc.vector.tensor_copy(rounded[g][:], source)
+        def interleave(group):
+            i0, columns, parts = GROUPS[group]
+            rounded[group] = held.tile([P, columns, PACK], BF16, name="rounded%d" % group, align_bytes=64)
+            source = picked[group][:].rearrange("p t i -> p i t")
+            if group == last:
+                nc.vector.tensor_copy(rounded[group][:], source)
             else:
-                nc.scalar.copy(rounded[g][:], source)
+                nc.scalar.copy(rounded[group][:], source)
 
-        def finish(g):
-            c0, n = groups[g]
-            codes = held.tile([P, n * CHUNK], U32, name="codes%d" % g, align_bytes=64)
-            plane = held.tile([P, n * CHUNK], U8, name="plane%d" % g, align_bytes=64)
-            nc.vector.quantize_mx(out=codes[:].bitcast(E4M3), scales=plane[:], in_=rounded[g][:].rearrange("p i t -> p (i t)"))
-            for c in range(c0, c0 + n):
-                cols = slice((c - c0) * CHUNK, (c - c0 + 1) * CHUNK)
-                for part, (acc, m0, count) in enumerate(accs[c]):
-                    for m in range(m0, m0 + count):
+        def finish(group):
+            i0, columns, parts = GROUPS[group]
+            ms_w = held.tile([P, columns], U32, name="ms_w%d" % group, align_bytes=64)
+            ms_s = held.tile([P, columns], U8, name="ms_s%d" % group, align_bytes=64)
+            nc.vector.quantize_mx(out=ms_w[:].bitcast(E4M3), scales=ms_s[:], in_=rounded[group][:].rearrange("p i t -> p (i t)"))
+            for m0, blocks in parts:
+                acc = sums[(group, m0)]
+                for m in range(m0, m0 + blocks):
+                    for c0 in range(0, columns, WIDTH):
                         nc.tensor.matmul_mx(
-                            out=acc[:, m - m0, :],
+                            out=acc[:, m - m0, c0 : c0 + WIDTH],
                             lhsT=wm_w[:, 2 * m * P : 2 * (m + 1) * P].bitcast(E2M1),
                             lhsT_scale=wm_s[:, m * P : (m + 1) * P],
-                            rhs=codes[:, cols].bitcast(E4M3),
-                            rhs_scale=plane[:, cols],
+                            rhs=ms_w[:, c0 : c0 + WIDTH].bitcast(E4M3),
+                            rhs_scale=ms_s[:, c0 : c0 + WIDTH],
                             start=False,
-                            stop=(m == m0 + count - 1),
+                            stop=(m == m0 + blocks - 1 and c0 + WIDTH == columns),
                         )
-                    result = held.tile([P, count, CHUNK], F32, name="result%d_%d" % (c, m0), align_bytes=64)
-                    target = out_rows[:, m0 : m0 + count, c * CHUNK : (c + 1) * CHUNK]
-                    if g == last and part == 0:
-                        nc.scalar.copy(result[:], acc[:])
-                        nc.scalar.dma_start(out=target, in_=result[:])
-                    elif g == last:
-                        nc.vector.tensor_copy(result[:], acc[:])
-                        nc.sync.dma_start(out=target, in_=result[:])
-                    else:
-                        nc.scalar.copy(result[:], acc[:])
-                        nc.sync.dma_start(out=target, in_=result[:])
+                result = held.tile([P, blocks, columns], F32, name="result%d_%d" % (group, m0), align_bytes=64)
+                target = out_rows[:, m0 : m0 + blocks, i0 : i0 + columns]
+                if group == last and m0 > 0:
+                    nc.vector.tensor_copy(result[:], acc[:])
+                else:
+                    nc.scalar.copy(result[:], acc[:])
+                queue = nc.scalar if group == last and m0 == 0 else nc.sync
+                queue.dma_start(out=target, in_=result[:])
 
         gather(0)
-        weave(0)
-        for g in range(1, last + 1):
-            gather(g)
-            if g < last:
-                weave(g)
-            finish(g - 1)
-        weave(last)
+        interleave(0)
+        for group in range(1, last):
+            gather(group)
+            interleave(group)
+            finish(group - 1)
+        gather(last)
+        finish(last - 1)
+        interleave(last)
         finish(last)

from contextlib import ExitStack

import concourse.mybir as mybir

K, T, J, I, N, M, L = 1024, 1024, 512, 512, 512, 512, 512
FLOPS = 2 * (K * N * J + N * M * I + L * M * I)

F32 = mybir.dt.float32
BF16 = mybir.dt.bfloat16
I32 = mybir.dt.int32
U32 = mybir.dt.uint32
U16 = mybir.dt.uint16
U8 = mybir.dt.uint8
E4M3 = mybir.dt.float8_e4m3fn_x4
E2M1 = mybir.dt.float4_e2m1fn_x4
RELU = mybir.ActivationFunctionType.Relu

P = 128
PACK = 4
PASSES = K // (P * PACK)
QUADRANT = 32
LIVE = 4
PER_COLUMN = 16
WIDTH = 128
LEAD = WIDTH
STAGE1_BANKS = 2
STAGED = 2

PIECES = [(t, 0, LEAD) for t in range(PACK - 1)] + [(t, LEAD, J - LEAD) for t in range(PACK - 1)] + [(PACK - 1, 0, J)]

GROUPS = [(0, 2 * WIDTH, [(0, 2), (2, 2)]), (2 * WIDTH, WIDTH, [(0, 4)]), (3 * WIDTH, WIDTH, [(0, 2), (2, 1), (3, 1)])]


def entries(offsets, first, count):
    return offsets[:, first // PER_COLUMN : (first + count) // PER_COLUMN]


def tile_list_expert_messages_kernel(
    tc, xq_words, xq_scales, wa_words, wa_scales, xi_words, xi_scales, wi_words, wi_scales, wm_words, wm_scales, offs, offs2, out
):
    nc = tc.nc
    quadrants = range(P // QUADRANT)
    with ExitStack() as ctx:
        held = ctx.enter_context(tc.tile_pool(name="held", bufs=1))
        ring = ctx.enter_context(tc.tile_pool(name="ring", bufs=STAGED))
        psum = ctx.enter_context(tc.psum_pool(name="psum", bufs=1))

        list1 = held.tile([P, J // PER_COLUMN], U16, name="list1")
        list2 = held.tile([P, I // PER_COLUMN], U16, name="list2")
        nc.sync.dma_start(list1[:], offs)

        xq_s = held.tile([P, T], U8, name="xq_s", align_bytes=64)
        nc.gpsimd.memset(xq_s[:].bitcast(I32), 0)
        wa_s_raw = held.tile([P, PASSES * N], U8, name="wa_s_raw", tag="narrow", align_bytes=64)
        nc.gpsimd.memset(wa_s_raw[:].bitcast(I32), 0)
        for g in quadrants:
            nc.sync.dma_start(
                out=xq_s[QUADRANT * g : QUADRANT * g + PASSES * LIVE, :].bitcast(I32),
                in_=xq_scales[:, LIVE * g : LIVE * (g + 1), :].bitcast(I32),
            )
        nc.sync.dma_start(list2[:], offs2)
        wa_w_raw = held.tile([P, PASSES * 2 * N], U8, name="wa_w_raw", align_bytes=64)
        nc.sync.dma_start(
            out=wa_w_raw[:].bitcast(I32).rearrange("p (z c) -> p z c", z=PASSES),
            in_=wa_words.bitcast(I32).rearrange("z p c -> p z c"),
        )
        xq_w = []
        for z in range(PASSES):
            window = held.tile([P, T], I32, name="xq_w%d" % z, tag="wide%d" % z, align_bytes=64)
            nc.sync.dma_start(out=window[:], in_=xq_words[z].rearrange("p n t -> p (n t)").bitcast(I32))
            xq_w.append(window)
        for g in quadrants:
            nc.sync.dma_start(
                out=wa_s_raw[QUADRANT * g : QUADRANT * g + LIVE, :].bitcast(I32).rearrange("r (z c) -> r z c", z=PASSES),
                in_=wa_scales[:, LIVE * g : LIVE * (g + 1), :].bitcast(I32).rearrange("z r c -> r z c"),
            )

        pages = []
        for t in range(PACK):
            page = held.tile([P, T], F32, name="page%d" % t, align_bytes=64)
            nc.vector.memset(page[:].bitcast(I32), 0)
            pages.append(page)

        xg_s0 = held.tile([P, J], U8, name="xg_s0", align_bytes=64)
        xg_s1 = held.tile([P, J], U8, name="xg_s1", align_bytes=64)
        nc.vector.tensor_copy(xg_s0[:], xq_s[:].indirect(list1[:]))
        for first, rows in ((0, 2 * QUADRANT), (2 * QUADRANT, LIVE), (3 * QUADRANT, LIVE)):
            nc.sync.dma_start(
                out=xg_s1[first : first + rows, :].bitcast(I32), in_=xg_s0[first + LIVE : first + LIVE + rows, :].bitcast(I32)
            )
        xg_s = [xg_s0, xg_s1]

        wa_w = held.tile([P, PASSES * 2 * N], U8, name="wa_w", align_bytes=64)
        nc.vector.tensor_copy(
            wa_w[:].bitcast(U16).rearrange("p (z t c) -> p z t c", z=PASSES, t=PACK),
            wa_w_raw[:].bitcast(U16).rearrange("p (z c t) -> p z t c", z=PASSES, t=PACK),
        )

        xg_lead = held.tile([P, J + LEAD], U32, name="xg_lead", align_bytes=64)
        nc.vector.tensor_copy(xg_lead[:, 0:J], xq_w[0][:].bitcast(U32).indirect(list1[:]))
        nc.vector.tensor_copy(xg_lead[:, J : J + LEAD], xq_w[1][:].bitcast(U32).indirect(entries(list1, 0, LEAD)))
        by_slice = wa_s_raw[:].rearrange("p (z c t) -> p z t c", z=PASSES, t=PACK)
        wa_s_first = held.tile([P, PASSES, 1, P], U8, name="wa_s_first", align_bytes=64)
        nc.vector.tensor_copy(wa_s_first[:], by_slice[:, :, 0:1, :])
        wa_s_rest = held.tile([P, PASSES, PACK - 1, P], U8, name="wa_s_rest", align_bytes=64)
        nc.vector.tensor_copy(wa_s_rest[:], by_slice[:, :, 1:PACK, :])
        xg_rest = held.tile([P, J - LEAD], U32, name="xg_rest", tag="narrow", align_bytes=64)
        nc.vector.tensor_copy(xg_rest[:], xq_w[1][:].bitcast(U32).indirect(entries(list1, LEAD, J - LEAD)))

        def xg_words(z, j0):
            if z == 1 and j0 >= LEAD:
                return xg_rest[:, j0 - LEAD : j0 - LEAD + WIDTH]
            return xg_lead[:, z * J + j0 : z * J + j0 + WIDTH]

        for b, (t, first, count) in enumerate(PIECES):
            acc = psum.tile([P, count], F32, name="p_acc%d" % b, tag="bank%d" % (b % STAGE1_BANKS))
            for z in range(PASSES):
                column = (z * PACK + t) * P
                for c0 in range(0, count, WIDTH):
                    nc.tensor.matmul_mx(
                        out=acc[:, c0 : c0 + WIDTH],
                        lhsT=wa_w[:, 2 * column : 2 * (column + P)].bitcast(E2M1),
                        lhsT_scale=wa_s_first[:, z, 0, :] if t == 0 else wa_s_rest[:, z, t - 1, :],
                        rhs=xg_words(z, first + c0).bitcast(E4M3),
                        rhs_scale=xg_s[z][:, first + c0 : first + c0 + WIDTH],
                        start=(z == 0 and c0 == 0),
                        stop=(z == PASSES - 1 and c0 + WIDTH == count),
                    )
            if b < len(PIECES) - STAGED:
                pr = held.tile([P, count], F32, name="pr%d" % b, align_bytes=64)
            else:
                pr = ring.tile([P, count], F32, name="pr%d" % b, tag="staged", align_bytes=64)
            nc.scalar.activation(pr[:], acc[:], RELU)
            nc.vector.tensor_copy(pages[t][:].indirect(entries(list1, first, count)), pr[:])

        late_s = held.tile([P, M + I + M], U8, name="late_s", tag="narrow", align_bytes=64)
        late_w = held.tile([P, 4 * M + 2 * I + 2 * M], U8, name="late_w", tag="wide0", align_bytes=64)
        wi_w, xi_w, wm_w = late_w[:, 0 : 4 * M], late_w[:, 4 * M : 4 * M + 2 * I], late_w[:, 4 * M + 2 * I : 6 * M + 2 * I]
        wi_s, xi_s, wm_s = late_s[:, 0:M], late_s[:, M : M + I], late_s[:, M + I : 2 * M + I]
        nc.sync.dma_start(out=wi_w.bitcast(I32), in_=wi_words[0].rearrange("p n t -> p (n t)").bitcast(I32))
        nc.sync.dma_start(out=xi_w.bitcast(I32), in_=xi_words[0].bitcast(I32))
        nc.sync.dma_start(out=wm_w.bitcast(I32), in_=wm_words[0].bitcast(I32))
        for plane, rows in ((wi_s, wi_scales[0]), (xi_s, xi_scales[0]), (wm_s, wm_scales[0])):
            for g in quadrants:
                nc.sync.dma_start(
                    out=plane[QUADRANT * g : QUADRANT * g + LIVE].bitcast(I32), in_=rows[LIVE * g : LIVE * (g + 1)].bitcast(I32)
                )

        sums = {}
        for group, (i0, columns, parts) in enumerate(GROUPS):
            for m0, blocks in parts:
                bank = STAGE1_BANKS + len(sums)
                acc = psum.tile([P, blocks, columns], F32, name="y_acc%d" % bank, tag="bank%d" % bank)
                sums[(group, m0)] = acc
                for m in range(m0, m0 + blocks):
                    for c0 in range(0, columns, WIDTH):
                        nc.tensor.matmul_mx(
                            out=acc[:, m - m0, c0 : c0 + WIDTH],
                            lhsT=wi_w[:, 4 * m * P : 4 * (m + 1) * P].bitcast(E4M3),
                            lhsT_scale=wi_s[:, m * P : (m + 1) * P],
                            rhs=xi_w[:, 2 * (i0 + c0) : 2 * (i0 + c0 + WIDTH)].bitcast(E2M1),
                            rhs_scale=xi_s[:, i0 + c0 : i0 + c0 + WIDTH],
                            start=(m == m0 and c0 == 0),
                            stop=False,
                        )

        out_rows = out.rearrange("(m p) i -> p m i", p=P)
        last = len(GROUPS) - 1
        picked = {}
        rounded = {}

        def gather(group):
            i0, columns, parts = GROUPS[group]
            picked[group] = ring.tile([P, PACK, columns], F32, name="picked%d" % group, tag="staged", align_bytes=64)
            for t in range(PACK):
                nc.vector.tensor_copy(picked[group][:, t, :], pages[t][:].indirect(entries(list2, i0, columns)))

        def interleave(group):
            i0, columns, parts = GROUPS[group]
            rounded[group] = held.tile([P, columns, PACK], BF16, name="rounded%d" % group, align_bytes=64)
            source = picked[group][:].rearrange("p t i -> p i t")
            if group == last:
                nc.vector.tensor_copy(rounded[group][:], source)
            else:
                nc.scalar.copy(rounded[group][:], source)

        def finish(group):
            i0, columns, parts = GROUPS[group]
            ms_w = held.tile([P, columns], U32, name="ms_w%d" % group, align_bytes=64)
            ms_s = held.tile([P, columns], U8, name="ms_s%d" % group, align_bytes=64)
            nc.vector.quantize_mx(out=ms_w[:].bitcast(E4M3), scales=ms_s[:], in_=rounded[group][:].rearrange("p i t -> p (i t)"))
            for m0, blocks in parts:
                acc = sums[(group, m0)]
                for m in range(m0, m0 + blocks):
                    for c0 in range(0, columns, WIDTH):
                        nc.tensor.matmul_mx(
                            out=acc[:, m - m0, c0 : c0 + WIDTH],
                            lhsT=wm_w[:, 2 * m * P : 2 * (m + 1) * P].bitcast(E2M1),
                            lhsT_scale=wm_s[:, m * P : (m + 1) * P],
                            rhs=ms_w[:, c0 : c0 + WIDTH].bitcast(E4M3),
                            rhs_scale=ms_s[:, c0 : c0 + WIDTH],
                            start=False,
                            stop=(m == m0 + blocks - 1 and c0 + WIDTH == columns),
                        )
                result = held.tile([P, blocks, columns], F32, name="result%d_%d" % (group, m0), align_bytes=64)
                target = out_rows[:, m0 : m0 + blocks, i0 : i0 + columns]
                if group == last and m0 > 0:
                    nc.vector.tensor_copy(result[:], acc[:])
                else:
                    nc.scalar.copy(result[:], acc[:])
                queue = nc.scalar if group == last and m0 == 0 else nc.sync
                queue.dma_start(out=target, in_=result[:])

        gather(0)
        interleave(0)
        for group in range(1, last):
            gather(group)
            interleave(group)
            finish(group - 1)
        gather(last)
        finish(last - 1)
        interleave(last)
        finish(last)
